import numpy as np
import ml_dtypes


def mxq(x, axis, fmt="e4m3"):
    dtype, down = {"e4m3": (ml_dtypes.float8_e4m3fn, 7), "e5m2": (ml_dtypes.float8_e5m2, 14)}[fmt]
    v = np.moveaxis(np.asarray(x, np.float32).astype(ml_dtypes.bfloat16).astype(np.float64), axis, -1)
    blocks = v.reshape(v.shape[:-1] + (-1, 32))
    amax = np.abs(blocks).max(-1, keepdims=True)
    byte = np.maximum(np.where(amax > 0, np.frexp(amax)[1] - 1 + 127, 0) - down, 1)
    scale = np.exp2(byte - 127.0)
    codes = (blocks / scale).astype(np.float32).astype(dtype).astype(np.float64)
    return np.moveaxis((codes * scale).reshape(v.shape), -1, axis)


WIDE = False


def mx_kscale(k, group=512):
    if not WIDE:
        return np.ones(k)
    levels = np.array([18, -18])
    if group != 512:
        return np.exp2(np.random.permutation(np.resize(levels, k // group))).repeat(group)
    if k % 512:
        return np.exp2(np.random.permutation(np.resize(levels, k // 32))).repeat(32)
    a = np.empty((k // 512, 16))
    for p in range(k // 512):
        a[p, :8] = np.random.permutation(np.resize(levels, 8))
        for g in range(8):
            far = levels[np.abs(levels - a[p, g]) >= 10]
            a[p, g + 8] = far[np.random.randint(len(far))]
    return np.exp2(a.ravel()).repeat(32)


def f64(x):
    return np.asarray(x).astype(np.float64)


E2M1 = np.array([0.0, 0.5, 1.0, 1.5, 2.0, 3.0, 4.0, 6.0, -0.0, -0.5, -1.0, -1.5, -2.0, -3.0, -4.0, -6.0])


def pack_group(w):
    k, n = w.shape
    w = f64(np.asarray(w, np.float32).astype(ml_dtypes.bfloat16)).reshape(k // 32, 32, n)
    amax = np.abs(w).max(1)
    mant, ex = np.frexp(amax / 6.0)
    byte = np.clip(np.where(amax > 0, np.where(mant > 0.5, ex, ex - 1) + 127, 1), 1, 254)
    scaled = (w * np.exp2(127.0 - byte)[:, None, :]).reshape(k, n).astype(np.float32)
    c = np.ascontiguousarray(scaled.reshape(k // 4, 4, n).transpose(0, 2, 1)).astype(ml_dtypes.float4_e2m1fn).view(np.uint8) & 0xF
    return np.ascontiguousarray((c[..., 0::2] | (c[..., 1::2] << 4)).reshape(k // 4, 2 * n)), byte.astype(np.uint8)


def unpack_group(words, scales):
    p, n = words.shape[0], scales.shape[1]
    words = np.ascontiguousarray(words).reshape(p, n, 2)
    nib = np.empty((p, n, 4), np.uint8)
    nib[..., 0::2] = words & 0xF
    nib[..., 1::2] = words >> 4
    return E2M1[nib].transpose(0, 2, 1).reshape(4 * p, n) * np.repeat(np.exp2(scales.astype(np.float64) - 127.0), 32, axis=0)


def silu(v):
    return v / (1.0 + np.exp(-v))


G, D, M, N = 4, 128, 256, 512


def setup_inputs():
    n = np.random.standard_normal
    s = mx_kscale(D, 0)[:, None]
    w_ = [pack_group(w) for w in n((G, D, M)) / np.sqrt(D) / s]
    u_ = [pack_group(w) for w in n((G, D, M)) / np.sqrt(D) / s]
    return {
        "x": (n((G, D, N)) * s).astype(np.float32),
        "w_words": np.stack([w[0] for w in w_]),
        "w_scales": np.stack([w[1] for w in w_]),
        "u_words": np.stack([w[0] for w in u_]),
        "u_scales": np.stack([w[1] for w in u_]),
        "b": (0.5 * n((G, M, 1))).astype(np.float32),
        "r": n((G, M, N)).astype(np.float32),
    }


def reference(x, w_words, w_scales, u_words, u_scales, b, r):
    xq = mxq(f64(x), 1, "e4m3")
    h = np.stack([unpack_group(w_words[g], w_scales[g]) for g in range(G)]).transpose(0, 2, 1) @ xq
    g = np.stack([unpack_group(u_words[g], u_scales[g]) for g in range(G)]).transpose(0, 2, 1) @ xq
    h = h + f64(b)
    y = silu(h) * g
    y = y + f64(r)
    return y

@@ -1,0 +1,126 @@
+from contextlib import ExitStack
+
+import concourse.mybir as mybir
+
+G, D, M, N = 4, 128, 256, 512
+FLOPS = 2 * 2 * G * D * M * N
+
+F32 = mybir.dt.float32
+BF16 = mybir.dt.bfloat16
+I32 = mybir.dt.int32
+U32 = mybir.dt.uint32
+U8 = mybir.dt.uint8
+FP8X4 = mybir.dt.float8_e4m3fn_x4
+FP4X4 = mybir.dt.float4_e2m1fn_x4
+ACT = mybir.ActivationFunctionType
+ALU = mybir.AluOpType
+
+P = 128
+PACK = 4
+ROWS = 32
+HALVES = M // P
+SPLIT = 256
+DVE_B = 160
+POOL_TILES = 3
+POOL_EXTRA = 0
+
+
+def interleave(copy, grouped, raw, c0, c1):
+    copy(
+        out=grouped[:, c0:c1, :].rearrange("p (c i) j -> p c j i", i=4),
+        in_=raw[:, :, c0:c1].rearrange("p j (c i) -> p c j i", i=4),
+    )
+
+
+def tile_rows_gglu_silu_bias_res_kernel(tc, x, w_words, w_scales, u_words, u_scales, b, r, out):
+    nc = tc.nc
+    with ExitStack() as ctx:
+        keep = ctx.enter_context(tc.tile_pool(name="keep", bufs=1))
+        psum = ctx.enter_context(tc.psum_pool(name="psum", bufs=1))
+        ctx.enter_context(tc.manual_schedule())
+
+        x_rows = x.rearrange("g (p j) n -> (g p) j n", j=PACK)
+        widths = [SPLIT, N - SPLIT]
+        raw_a = keep.tile([P, PACK, widths[0]], F32)
+        raw_b = keep.tile([P, PACK, widths[1]], F32)
+        nc.sync.dma_start(out=raw_a[:], in_=x_rows[:, :, 0:SPLIT])
+        nc.sync.dma_start(out=raw_b[:], in_=x_rows[:, :, SPLIT:N])
+
+        planes = keep.tile([P, 2 * M], U8, align_bytes=64)
+        nc.vector.memset(planes[:].bitcast(I32), 0)
+        bias_rows = keep.tile([P, G * HALVES * ROWS], F32, align_bytes=64)
+        nc.vector.memset(bias_rows[:], 0.0)
+        warm = keep.tile([P, 1], F32)
+        nc.scalar.activation(out=warm[:], in_=bias_rows[:, 0:1], func=ACT.Silu)
+
+        weights = []
+        for k, words in enumerate((w_words, u_words)):
+            wt = keep.tile([P, 2 * M], U8, name="words%d" % k, align_bytes=64)
+            nc.sync.dma_start(out=wt[:].bitcast(I32), in_=words.rearrange("g p b -> (g p) b").bitcast(I32))
+            weights.append((wt, planes[:, k * M : (k + 1) * M]))
+        for g in range(G):
+            queue = nc.sync if g < 2 else nc.gpsimd
+            for k, scales in enumerate((w_scales, u_scales)):
+                queue.dma_start(out=planes[ROWS * g : ROWS * g + PACK, k * M : (k + 1) * M].bitcast(I32), in_=scales[g].bitcast(I32))
+        nc.sync.dma_start(
+            out=bias_rows[0:P:ROWS, :].rearrange("a (c i) -> a c i", i=ROWS),
+            in_=b.rearrange("g (h a i) o -> a (g h) (i o)", h=HALVES, i=ROWS),
+        )
+
+        order = [(g, h) for h in range(HALVES) for g in range(G)]
+        res = []
+        for t in range(0, len(order), 2):
+            g, h = order[t]
+            pair = keep.tile([P, 2, N], F32, name="res%d" % t)
+            nc.sync.dma_start(out=pair[:], in_=r[g : g + 2, h * P : (h + 1) * P, :].rearrange("g p n -> p g n"))
+            res.append(pair[:, 0, :])
+            res.append(pair[:, 1, :])
+
+        codes = keep.tile([P, N], U32, align_bytes=64)
+        xscales = keep.tile([P, N], U8, align_bytes=64)
+        grouped_a = keep.tile([P, widths[0], PACK], BF16, align_bytes=64)
+        grouped_b = keep.tile([P, widths[1], PACK], BF16, align_bytes=64)
+        bias = keep.tile([P, G * HALVES * ROWS], F32, align_bytes=64)
+
+        interleave(nc.vector.tensor_copy, grouped_a, raw_a, 0, widths[0])
+        nc.vector.quantize_mx(out=codes[:, 0:SPLIT].bitcast(FP8X4), scales=xscales[:, 0:SPLIT], in_=grouped_a[:].rearrange("p w j -> p (w j)"))
+        interleave(nc.vector.tensor_copy, grouped_b, raw_b, 0, DVE_B)
+        interleave(nc.scalar.copy, grouped_b, raw_b, DVE_B, widths[1])
+        nc.vector.quantize_mx(out=codes[:, SPLIT:N].bitcast(FP8X4), scales=xscales[:, SPLIT:N], in_=grouped_b[:].rearrange("p w j -> p (w j)"))
+        nc.vector.transpose(out=bias[:], in_=bias_rows[:])
+
+        banks = [[psum.tile([P, N], F32, name="bank%d_%d" % (g, k)) for k in range(2)] for g in range(G)]
+
+        def add_and_store(t, pool_cols):
+            g, h = order[t]
+            y = keep.tile([P, N], F32, name="y%d" % t)
+            if pool_cols > 0:
+                nc.gpsimd.tensor_tensor(out=y[:, 0:pool_cols], in0=prods[t][:, 0:pool_cols], in1=res[t][:, 0:pool_cols], op=ALU.add)
+            if pool_cols < N:
+                nc.vector.tensor_tensor(out=y[:, pool_cols:N], in0=prods[t][:, pool_cols:N], in1=res[t][:, pool_cols:N], op=ALU.add)
+            nc.sync.dma_start(out=out[g, h * P : (h + 1) * P, :], in_=y[:])
+
+        prods = []
+        for t, (g, h) in enumerate(order):
+            rows = slice(ROWS * g, ROWS * (g + 1))
+            for k in range(2):
+                wt, st = weights[k]
+                nc.tensor.matmul_mx(
+                    out=banks[g][k][:],
+                    lhsT=wt[rows, 2 * P * h : 2 * P * (h + 1)].bitcast(FP4X4),
+                    lhsT_scale=st[rows, P * h : P * (h + 1)],
+                    rhs=codes[rows, :].bitcast(FP8X4),
+                    rhs_scale=xscales[rows, :],
+                    start=True,
+                    stop=True,
+                )
+            act = keep.tile([P, N], F32, name="act%d" % t)
+            c = ROWS * (HALVES * g + h)
+            nc.scalar.activation(out=act[:], in_=banks[g][0][:], func=ACT.Silu, bias=bias[:, c : c + 1])
+            prod = keep.tile([P, N], F32, name="prod%d" % t)
+            nc.vector.tensor_tensor(out=prod[:], in0=banks[g][1][:], in1=act[:], op=ALU.mult)
+            prods.append(prod)
+            if t < POOL_TILES:
+                add_and_store(t, N)
+        for t in range(POOL_TILES, len(order)):
+            add_and_store(t, POOL_EXTRA if t == POOL_TILES else 0)

@@ -39,42 +39,54 @@ def tile_rows_gglu_silu_bias_res_kernel(tc, x, w_words, w_scales, u_words, u_sca
         psum = ctx.enter_context(tc.psum_pool(name="psum", bufs=1))
         ctx.enter_context(tc.manual_schedule())
 
+        order = [(g, h) for h in range(HALVES) for g in range(G)]
         x_rows = x.rearrange("g (p j) n -> (g p) j n", j=PACK)
         widths = [SPLIT, N - SPLIT]
         raw_a = keep.tile([P, PACK, widths[0]], F32)
         raw_b = keep.tile([P, PACK, widths[1]], F32)
-        nc.sync.dma_start(out=raw_a[:], in_=x_rows[:, :, 0:SPLIT])
-        nc.sync.dma_start(out=raw_b[:], in_=x_rows[:, :, SPLIT:N])
-
         planes = keep.tile([P, 2 * M], U8, align_bytes=64)
-        nc.vector.memset(planes[:].bitcast(I32), 0)
         bias_rows = keep.tile([P, G * HALVES * ROWS], F32, align_bytes=64)
+        words = [keep.tile([P, 2 * M], U8, name="words%d" % k, align_bytes=64) for k in range(2)]
+        nc.vector.memset(planes[:].bitcast(I32), 0)
         nc.vector.memset(bias_rows[:], 0.0)
         warm = keep.tile([P, 1], F32)
         nc.scalar.activation(out=warm[:], in_=bias_rows[:, 0:1], func=ACT.Silu)
 
-        weights = []
-        for k, words in enumerate((w_words, u_words)):
-            wt = keep.tile([P, 2 * M], U8, name="words%d" % k, align_bytes=64)
-            nc.sync.dma_start(out=wt[:].bitcast(I32), in_=words.rearrange("g p b -> (g p) b").bitcast(I32))
-            weights.append((wt, planes[:, k * M : (k + 1) * M]))
-        for g in range(G):
-            queue = nc.sync if g < 2 else nc.gpsimd
-            for k, scales in enumerate((w_scales, u_scales)):
-                queue.dma_start(out=planes[ROWS * g : ROWS * g + PACK, k * M : (k + 1) * M].bitcast(I32), in_=scales[g].bitcast(I32))
-        nc.sync.dma_start(
-            out=bias_rows[0:P:ROWS, :].rearrange("a (c i) -> a c i", i=ROWS),
-            in_=b.rearrange("g (h a i) o -> a (g h) (i o)", h=HALVES, i=ROWS),
-        )
+        def load_words(k):
+            src = (w_words, u_words)[k]
+            nc.sync.dma_start(out=words[k][:].bitcast(I32), in_=src.rearrange("g p b -> (g p) b").bitcast(I32))
 
-        order = [(g, h) for h in range(HALVES) for g in range(G)]
+        def load_scales(g, k):
+            src = (w_scales, u_scales)[k]
+            nc.sync.dma_start(out=planes[ROWS * g : ROWS * g + PACK, k * M : (k + 1) * M].bitcast(I32), in_=src[g].bitcast(I32))
+
         res = []
-        for t in range(0, len(order), 2):
+
+        def load_res(t):
             g, h = order[t]
             pair = keep.tile([P, 2, N], F32, name="res%d" % t)
             nc.sync.dma_start(out=pair[:], in_=r[g : g + 2, h * P : (h + 1) * P, :].rearrange("g p n -> p g n"))
             res.append(pair[:, 0, :])
             res.append(pair[:, 1, :])
+
+        nc.sync.dma_start(out=raw_a[:], in_=x_rows[:, :, 0:SPLIT])
+        nc.sync.dma_start(out=raw_b[:], in_=x_rows[:, :, SPLIT:N])
+        load_words(0)
+        load_scales(0, 0)
+        load_words(1)
+        load_scales(0, 1)
+        load_scales(1, 0)
+        nc.sync.dma_start(
+            out=bias_rows[0:P:ROWS, :].rearrange("a (c i) -> a c i", i=ROWS),
+            in_=b.rearrange("g (h a i) o -> a (g h) (i o)", h=HALVES, i=ROWS),
+        )
+        load_res(0)
+        load_scales(1, 1)
+        for g in range(2, G):
+            for k in range(2):
+                load_scales(g, k)
+        for t in range(2, len(order), 2):
+            load_res(t)
 
         codes = keep.tile([P, N], U32, align_bytes=64)
         xscales = keep.tile([P, N], U8, align_bytes=64)
@@ -91,6 +103,19 @@ def tile_rows_gglu_silu_bias_res_kernel(tc, x, w_words, w_scales, u_words, u_sca
 
         banks = [[psum.tile([P, N], F32, name="bank%d_%d" % (g, k)) for k in range(2)] for g in range(G)]
 
+        def product(t, k):
+            g, h = order[t]
+            rows = slice(ROWS * g, ROWS * (g + 1))
+            nc.tensor.matmul_mx(
+                out=banks[g][k][:],
+                lhsT=words[k][rows, 2 * P * h : 2 * P * (h + 1)].bitcast(FP4X4),
+                lhsT_scale=planes[rows, k * M + P * h : k * M + P * (h + 1)],
+                rhs=codes[rows, :].bitcast(FP8X4),
+                rhs_scale=xscales[rows, :],
+                start=True,
+                stop=True,
+            )
+
         def add_and_store(t, pool_cols):
             g, h = order[t]
             y = keep.tile([P, N], F32, name="y%d" % t)
@@ -101,24 +126,16 @@ def tile_rows_gglu_silu_bias_res_kernel(tc, x, w_words, w_scales, u_words, u_sca
             nc.sync.dma_start(out=out[g, h * P : (h + 1) * P, :], in_=y[:])
 
         prods = []
+        product(0, 0)
         for t, (g, h) in enumerate(order):
-            rows = slice(ROWS * g, ROWS * (g + 1))
-            for k in range(2):
-                wt, st = weights[k]
-                nc.tensor.matmul_mx(
-                    out=banks[g][k][:],
-                    lhsT=wt[rows, 2 * P * h : 2 * P * (h + 1)].bitcast(FP4X4),
-                    lhsT_scale=st[rows, P * h : P * (h + 1)],
-                    rhs=codes[rows, :].bitcast(FP8X4),
-                    rhs_scale=xscales[rows, :],
-                    start=True,
-                    stop=True,
-                )
+            if t + 1 < len(order):
+                product(t + 1, 0)
+            product(t, 1)
             act = keep.tile([P, N], F32, name="act%d" % t)
             c = ROWS * (HALVES * g + h)
             nc.scalar.activation(out=act[:], in_=banks[g][0][:], func=ACT.Silu, bias=bias[:, c : c + 1])
             prod = keep.tile([P, N], F32, name="prod%d" % t)
-            nc.vector.tensor_tensor(out=prod[:], in0=banks[g][1][:], in1=act[:], op=ALU.mult)
+            nc.vector.tensor_tensor(out=prod[:], in0=act[:], in1=banks[g][1][:], op=ALU.mult)
             prods.append(prod)
             if t < POOL_TILES:
                 add_and_store(t, N)

from contextlib import ExitStack

import concourse.mybir as mybir

G, D, M, N = 4, 128, 256, 512
FLOPS = 2 * 2 * G * D * M * N

F32 = mybir.dt.float32
BF16 = mybir.dt.bfloat16
I32 = mybir.dt.int32
U32 = mybir.dt.uint32
U8 = mybir.dt.uint8
FP8X4 = mybir.dt.float8_e4m3fn_x4
FP4X4 = mybir.dt.float4_e2m1fn_x4
ACT = mybir.ActivationFunctionType
ALU = mybir.AluOpType

P = 128
PACK = 4
ROWS = 32
HALVES = M // P
SPLIT = 256
DVE_B = 160
POOL_TILES = 3
POOL_EXTRA = 0


def interleave(copy, grouped, raw, c0, c1):
    copy(
        out=grouped[:, c0:c1, :].rearrange("p (c i) j -> p c j i", i=4),
        in_=raw[:, :, c0:c1].rearrange("p j (c i) -> p c j i", i=4),
    )


def tile_rows_gglu_silu_bias_res_kernel(tc, x, w_words, w_scales, u_words, u_scales, b, r, out):
    nc = tc.nc
    with ExitStack() as ctx:
        keep = ctx.enter_context(tc.tile_pool(name="keep", bufs=1))
        psum = ctx.enter_context(tc.psum_pool(name="psum", bufs=1))
        ctx.enter_context(tc.manual_schedule())

        order = [(g, h) for h in range(HALVES) for g in range(G)]
        x_rows = x.rearrange("g (p j) n -> (g p) j n", j=PACK)
        widths = [SPLIT, N - SPLIT]
        raw_a = keep.tile([P, PACK, widths[0]], F32)
        raw_b = keep.tile([P, PACK, widths[1]], F32)
        planes = keep.tile([P, 2 * M], U8, align_bytes=64)
        bias_rows = keep.tile([P, G * HALVES * ROWS], F32, align_bytes=64)
        words = [keep.tile([P, 2 * M], U8, name="words%d" % k, align_bytes=64) for k in range(2)]
        nc.vector.memset(planes[:].bitcast(I32), 0)
        nc.vector.memset(bias_rows[:], 0.0)
        warm = keep.tile([P, 1], F32)
        nc.scalar.activation(out=warm[:], in_=bias_rows[:, 0:1], func=ACT.Silu)

        def load_words(k):
            src = (w_words, u_words)[k]
            nc.sync.dma_start(out=words[k][:].bitcast(I32), in_=src.rearrange("g p b -> (g p) b").bitcast(I32))

        def load_scales(g, k):
            src = (w_scales, u_scales)[k]
            nc.sync.dma_start(out=planes[ROWS * g : ROWS * g + PACK, k * M : (k + 1) * M].bitcast(I32), in_=src[g].bitcast(I32))

        res = []

        def load_res(t):
            g, h = order[t]
            pair = keep.tile([P, 2, N], F32, name="res%d" % t)
            nc.sync.dma_start(out=pair[:], in_=r[g : g + 2, h * P : (h + 1) * P, :].rearrange("g p n -> p g n"))
            res.append(pair[:, 0, :])
            res.append(pair[:, 1, :])

        nc.sync.dma_start(out=raw_a[:], in_=x_rows[:, :, 0:SPLIT])
        nc.sync.dma_start(out=raw_b[:], in_=x_rows[:, :, SPLIT:N])
        load_words(0)
        load_scales(0, 0)
        load_words(1)
        load_scales(0, 1)
        load_scales(1, 0)
        nc.sync.dma_start(
            out=bias_rows[0:P:ROWS, :].rearrange("a (c i) -> a c i", i=ROWS),
            in_=b.rearrange("g (h a i) o -> a (g h) (i o)", h=HALVES, i=ROWS),
        )
        load_res(0)
        load_scales(1, 1)
        for g in range(2, G):
            for k in range(2):
                load_scales(g, k)
        for t in range(2, len(order), 2):
            load_res(t)

        codes = keep.tile([P, N], U32, align_bytes=64)
        xscales = keep.tile([P, N], U8, align_bytes=64)
        grouped_a = keep.tile([P, widths[0], PACK], BF16, align_bytes=64)
        grouped_b = keep.tile([P, widths[1], PACK], BF16, align_bytes=64)
        bias = keep.tile([P, G * HALVES * ROWS], F32, align_bytes=64)

        interleave(nc.vector.tensor_copy, grouped_a, raw_a, 0, widths[0])
        nc.vector.quantize_mx(out=codes[:, 0:SPLIT].bitcast(FP8X4), scales=xscales[:, 0:SPLIT], in_=grouped_a[:].rearrange("p w j -> p (w j)"))
        interleave(nc.vector.tensor_copy, grouped_b, raw_b, 0, DVE_B)
        interleave(nc.scalar.copy, grouped_b, raw_b, DVE_B, widths[1])
        nc.vector.quantize_mx(out=codes[:, SPLIT:N].bitcast(FP8X4), scales=xscales[:, SPLIT:N], in_=grouped_b[:].rearrange("p w j -> p (w j)"))
        nc.vector.transpose(out=bias[:], in_=bias_rows[:])

        banks = [[psum.tile([P, N], F32, name="bank%d_%d" % (g, k)) for k in range(2)] for g in range(G)]

        def product(t, k):
            g, h = order[t]
            rows = slice(ROWS * g, ROWS * (g + 1))
            nc.tensor.matmul_mx(
                out=banks[g][k][:],
                lhsT=words[k][rows, 2 * P * h : 2 * P * (h + 1)].bitcast(FP4X4),
                lhsT_scale=planes[rows, k * M + P * h : k * M + P * (h + 1)],
                rhs=codes[rows, :].bitcast(FP8X4),
                rhs_scale=xscales[rows, :],
                start=True,
                stop=True,
            )

        def add_and_store(t, pool_cols):
            g, h = order[t]
            y = keep.tile([P, N], F32, name="y%d" % t)
            if pool_cols > 0:
                nc.gpsimd.tensor_tensor(out=y[:, 0:pool_cols], in0=prods[t][:, 0:pool_cols], in1=res[t][:, 0:pool_cols], op=ALU.add)
            if pool_cols < N:
                nc.vector.tensor_tensor(out=y[:, pool_cols:N], in0=prods[t][:, pool_cols:N], in1=res[t][:, pool_cols:N], op=ALU.add)
            nc.sync.dma_start(out=out[g, h * P : (h + 1) * P, :], in_=y[:])

        prods = []
        product(0, 0)
        for t, (g, h) in enumerate(order):
            if t + 1 < len(order):
                product(t + 1, 0)
            product(t, 1)
            act = keep.tile([P, N], F32, name="act%d" % t)
            c = ROWS * (HALVES * g + h)
            nc.scalar.activation(out=act[:], in_=banks[g][0][:], func=ACT.Silu, bias=bias[:, c : c + 1])
            prod = keep.tile([P, N], F32, name="prod%d" % t)
            nc.vector.tensor_tensor(out=prod[:], in0=act[:], in1=banks[g][1][:], op=ALU.mult)
            prods.append(prod)
            if t < POOL_TILES:
                add_and_store(t, N)
        for t in range(POOL_TILES, len(order)):
            add_and_store(t, POOL_EXTRA if t == POOL_TILES else 0)
